import numpy as np
import ml_dtypes


def mxq(x, axis, fmt="e4m3"):
    dtype, down = {"e4m3": (ml_dtypes.float8_e4m3fn, 7), "e5m2": (ml_dtypes.float8_e5m2, 14)}[fmt]
    v = np.moveaxis(np.asarray(x, np.float32).astype(ml_dtypes.bfloat16).astype(np.float64), axis, -1)
    blocks = v.reshape(v.shape[:-1] + (-1, 32))
    amax = np.abs(blocks).max(-1, keepdims=True)
    byte = np.maximum(np.where(amax > 0, np.frexp(amax)[1] - 1 + 127, 0) - down, 1)
    scale = np.exp2(byte - 127.0)
    codes = (blocks / scale).astype(np.float32).astype(dtype).astype(np.float64)
    return np.moveaxis((codes * scale).reshape(v.shape), -1, axis)


WIDE = False


def mx_kscale(k):
    if not WIDE:
        return np.ones(k)
    levels = np.array([10, -10, 5, -5, 0])
    if k % 512:
        return np.exp2(np.random.permutation(np.resize(levels, k // 32))).repeat(32)
    a = np.empty((k // 512, 16))
    for p in range(k // 512):
        a[p, :8] = np.random.permutation(np.resize(levels, 8))
        for g in range(8):
            far = levels[np.abs(levels - a[p, g]) >= 10]
            a[p, g + 8] = far[np.random.randint(len(far))]
    return np.exp2(a.ravel()).repeat(32)


def f64(x):
    return np.asarray(x).astype(np.float64)


def striped(idx):
    return np.tile(np.asarray(idx).reshape(-1, 16).T, (8, 1)).astype(np.uint16)


def unstriped(offs):
    return offs[:16].T.reshape(-1).astype(np.int64)


E2M1 = np.array([0.0, 0.5, 1.0, 1.5, 2.0, 3.0, 4.0, 6.0, -0.0, -0.5, -1.0, -1.5, -2.0, -3.0, -4.0, -6.0])


def pack_weight(w, fmt):
    k, n = w.shape
    w = f64(np.asarray(w, np.float32).astype(ml_dtypes.bfloat16)).reshape(k // 32, 32, n)
    amax = np.abs(w).max(1)
    if fmt == "e4m3":
        byte = np.frexp(amax)[1] - 1 + 127 - 7
    else:
        mant, ex = np.frexp(amax / 6.0)
        byte = np.where(mant > 0.5, ex, ex - 1) + 127
    byte = np.clip(np.where(amax > 0, byte, 1), 1, 254)
    scaled = (w * np.exp2(127.0 - byte)[:, None, :]).reshape(k, n).astype(np.float32)
    by_word = np.ascontiguousarray(scaled.reshape(k // 512, 128, 4, n).transpose(0, 1, 3, 2))
    if fmt == "e4m3":
        words = by_word.astype(ml_dtypes.float8_e4m3fn).view(np.uint8)
    else:
        c = by_word.astype(ml_dtypes.float4_e2m1fn).view(np.uint8) & 0xF
        words = (c[..., 0::2] | (c[..., 1::2] << 4)).reshape(k // 512, 128, 2 * n)
    return np.ascontiguousarray(words), np.ascontiguousarray(byte.astype(np.uint8).reshape(k // 512, 16, n))


def unpack_weight(words, scales, fmt):
    g, _, n = scales.shape
    words = np.ascontiguousarray(words).reshape(g, 128, n, -1)
    if fmt == "e4m3":
        vals = words.view(ml_dtypes.float8_e4m3fn).astype(np.float64)
    else:
        nib = np.empty((g, 128, n, 4), np.uint8)
        nib[..., 0::2] = words & 0xF
        nib[..., 1::2] = words >> 4
        vals = E2M1[nib]
    vals = vals * np.repeat(np.exp2(scales.astype(np.float64) - 127.0), 8, axis=1)[..., None]
    return vals.transpose(0, 1, 3, 2).reshape(g * 512, n)


def sigmoid(v):
    return 1.0 / (1.0 + np.exp(-v))


D, E, T, I, Q = 512, 512, 2048, 512, 128


def setup_inputs():
    n = np.random.standard_normal
    idx = np.random.permutation(T)[:I]
    fd = mx_kscale(D)
    fi = mx_kscale(I)
    ti = np.ones(T)
    ti[idx] = fi
    keysp = pack_weight(n((D, T)) / fd[:, None], "e4m3")
    return {
        "query": (n((D, Q)) * 0.5 / np.sqrt(D) * fd[:, None]).astype(np.float32),
        "query2": (n((D, Q)) * 1.2 / np.sqrt(D) * fd[:, None]).astype(np.float32),
        "dquery2": (n((D, Q)) * 1.0 / np.sqrt(D) * fd[:, None]).astype(np.float32),
        "keys_words": keysp[0],
        "keys_scales": keysp[1],
        "os": (np.random.uniform(4.0, 16.0, (1, I)) * fi).astype(np.float32),
        "vals": (n((E, T)) / ti).astype(np.float32),
        "offs": striped(idx),
    }


def reference(query, query2, dquery2, keys_words, keys_scales, os, vals, offs):
    idx = unstriped(offs)
    keysu = unpack_weight(keys_words, keys_scales, "e4m3")
    queryq = mxq(f64(query), 0, "e4m3")
    keysidxg = keysu[:, idx]
    a = queryq.T @ keysidxg
    query2q = mxq(f64(query2), 0, "e4m3")
    b = query2q.T @ keysidxg
    dquery2q = mxq(f64(dquery2), 0, "e4m3")
    tb = dquery2q.T @ keysidxg
    r = np.exp(a - np.max(a, axis=1, keepdims=True))
    gt = sigmoid(b)
    p = r * gt
    tgt = tb * gt * (1.0 - gt)
    tp = tgt * r
    tw = (tp - np.sum(tp, axis=1, keepdims=True) * p / np.sum(p, axis=1, keepdims=True)) / np.sum(p, axis=1, keepdims=True)
    wo1 = tw * f64(os)
    wt1 = wo1.T
    vt1 = f64(vals)[:, idx].T
    wt1q = mxq(wt1, 0, "e4m3")
    vt1q = mxq(vt1, 0, "e4m3")
    o = wt1q.T @ vt1q
    return o

@@ -1,0 +1,174 @@
+from contextlib import ExitStack
+
+import concourse.mybir as mybir
+from concourse.masks import make_identity
+
+D, E, T, I, Q = 512, 512, 2048, 512, 128
+FLOPS = 2 * Q * I * D * 3 + 2 * Q * I * E
+
+F32 = mybir.dt.float32
+BF16 = mybir.dt.bfloat16
+I32 = mybir.dt.int32
+U32 = mybir.dt.uint32
+U16 = mybir.dt.uint16
+U8 = mybir.dt.uint8
+FP8X4 = mybir.dt.float8_e4m3fn_x4
+ALU = mybir.AluOpType
+ACT = mybir.ActivationFunctionType
+
+P = 128
+PACK = 4
+CHUNKS = E // P
+
+
+def tile_attend_ttgatedexp_kernel(tc, query, query2, dquery2, keys_words, keys_scales, slot_os, vals, offs, out):
+    nc = tc.nc
+    with ExitStack() as ctx:
+        sb = ctx.enter_context(tc.tile_pool(name="sb", bufs=1))
+        ps = ctx.enter_context(tc.psum_pool(name="ps", bufs=1))
+
+        offsets = sb.tile([P, I // 16], U16, name="offsets")
+        key_words = sb.tile([P, T], I32, name="key_words", tag="slot0", align_bytes=64)
+        key_scales = sb.tile([P, T], U8, name="key_scales")
+        warm_out = sb.tile([P, 1], F32, name="warm_out")
+
+        nc.gpsimd.memset(key_scales[:].bitcast(I32), 0)
+        nc.sync.dma_start(offsets[:], offs)
+        for quad in range(4):
+            nc.scalar.dma_start(
+                key_scales[32 * quad : 32 * quad + 4, :].bitcast(I32),
+                keys_scales[0, 4 * quad : 4 * quad + 4, :].bitcast(I32),
+            )
+        def load_queries(pool, n, rows):
+            raw = pool.tile([P, PACK, Q], F32, name=f"q_raw{n}")
+            nc.sync.dma_start(raw[:], rows.rearrange("(p j) q -> p j q", j=PACK))
+            return raw
+
+        nc.sync.dma_start(key_words[:], keys_words[0].rearrange("p n t -> p (n t)").bitcast(I32))
+        q_raw = [load_queries(sb, 0, query2)]
+        with tc.tile_pool(name="head", bufs=1) as head:
+            warm = head.tile([P, 1], F32, name="warm")
+            nc.gpsimd.memset(warm[:], 0.0)
+            nc.scalar.activation(warm_out[:], warm[:], ACT.Sigmoid)
+        later = ctx.enter_context(tc.tile_pool(name="later", bufs=1))
+        q_raw.append(load_queries(later, 1, query))
+        q_raw.append(load_queries(later, 2, dquery2))
+        slot_factor = later.tile([P, PACK], F32, name="slot_factor")
+        nc.sync.dma_start(slot_factor[:], slot_os[0].rearrange("(p t) -> p t", t=PACK))
+        v_raw = []
+        for c in range(CHUNKS):
+            raw = later.tile([P, T], F32, name=f"v_raw{c}")
+            nc.sync.dma_start(raw[:], vals[P * c : P * (c + 1), :])
+            v_raw.append(raw)
+
+        ident = sb.tile([P, P], F32, name="ident")
+        make_identity(nc, ident[:])
+
+        k_scales = sb.tile([P, I], U8, name="k_scales", align_bytes=64)
+        nc.vector.tensor_copy(k_scales[:], key_scales[:].indirect(offsets[:]))
+        k_codes = sb.tile([P, I], U32, name="k_codes", align_bytes=64)
+        nc.vector.tensor_copy(k_codes[:], key_words[:].bitcast(U32).indirect(offsets[:]))
+
+        q_codes = sb.tile([P, 3, Q], U32, name="q_codes", tag="slot0", align_bytes=64)
+        scores = []
+        for n in range(3):
+            grouped = sb.tile([P, Q, PACK], BF16, name=f"q_grouped{n}", align_bytes=64)
+            nc.scalar.copy(grouped[:], q_raw[n][:].rearrange("p j q -> p q j"))
+            codes = q_codes[:, n, :]
+            scales = sb.tile([P, Q], U8, name=f"q_scales{n}", align_bytes=64)
+            nc.vector.quantize_mx(out=codes.bitcast(FP8X4), scales=scales[:], in_=grouped[:].rearrange("p q j -> p (q j)"))
+            bank = ps.tile([P, I], F32, name=f"score{n}", tag=f"score{n}")
+            nc.tensor.matmul_mx(
+                out=bank[:], lhsT=codes.bitcast(FP8X4), lhsT_scale=scales[:],
+                rhs=k_codes[:].bitcast(FP8X4), rhs_scale=k_scales[:], start=True, stop=True,
+            )
+            scores.append(bank)
+        b_ps, a_ps, tb_ps = scores
+
+        def dealt(bank):
+            return bank[:].rearrange("q (s t) -> q t s", t=PACK)
+
+        first_pair = sb.tile([P, 2, P * PACK], BF16, name="first_pair", align_bytes=64)
+        v_grouped = [first_pair[:, 0, :], first_pair[:, 1, :]]
+        for c in range(2, CHUNKS):
+            single = sb.tile([P, P * PACK], BF16, name=f"v_grouped{c}", align_bytes=64)
+            v_grouped.append(single[:])
+
+        def gather_values(c):
+            picked = sb.tile([P, I], BF16, name=f"v_picked{c}", tag=f"slot{c}", align_bytes=64)
+            nc.vector.tensor_copy(picked[:], v_raw[c][:].indirect(offsets[:]))
+            pairs = picked[:].bitcast(F32)
+            turned = ps.tile([P, 2, P], F32, name=f"v_turned{c}", tag=f"v_turned{c % 2}")
+            for u in range(2):
+                nc.tensor.transpose(turned[:, u, :], pairs[:, u : I // 2 : 2], ident[:])
+            nc.scalar.copy(
+                v_grouped[c].bitcast(F32).rearrange("p (e u) -> p e u", u=2),
+                turned[:].rearrange("p u e -> p e u"),
+            )
+
+        gt = sb.tile([P, PACK, P], F32, name="gt")
+        nc.scalar.activation(gt[:], dealt(b_ps), ACT.Sigmoid)
+        neg_max = sb.tile([P, 1], F32, name="neg_max")
+        nc.vector.tensor_reduce(neg_max[:], a_ps[:], mybir.AxisListType.X, ALU.max, negate=True)
+        neg_u = sb.tile([P, PACK, P], F32, name="neg_u", tag="slot1", align_bytes=64)
+        nc.vector.scalar_tensor_tensor(neg_u[:], gt[:], 1.0, dealt(tb_ps), ALU.subtract, ALU.mult)
+        r = sb.tile([P, PACK, P], F32, name="r")
+        nc.scalar.activation(r[:], dealt(a_ps), ACT.Exp, bias=neg_max[:])
+        gather_values(0)
+        p = sb.tile([P, PACK, P], F32, name="p")
+        p_sum = sb.tile([P, 1], F32, name="p_sum")
+        nc.vector.scalar_tensor_tensor(p[:], r[:], 1.0, gt[:], ALU.mult, ALU.mult, accum_out=p_sum[:])
+        inv_sum = sb.tile([P, 1], F32, name="inv_sum")
+        nc.vector.reciprocal(inv_sum[:], p_sum[:])
+        p_norm = sb.tile([P, PACK, P], F32, name="p_norm", tag="slot3", align_bytes=64)
+        nc.scalar.activation(p_norm[:], p[:], ACT.Copy, scale=inv_sum[:])
+        neg_tp = sb.tile([P, PACK, P], F32, name="neg_tp", tag="slot2", align_bytes=64)
+        neg_c = sb.tile([P, 1], F32, name="neg_c", tag="slot4", align_bytes=64)
+        nc.vector.scalar_tensor_tensor(neg_tp[:], p[:], inv_sum[:], neg_u[:], ALU.mult, ALU.mult, accum_out=neg_c[:])
+        gather_values(1)
+        tw = sb.tile([P, PACK, P], F32, name="tw")
+        nc.vector.scalar_tensor_tensor(tw[:], p_norm[:], neg_c[:], neg_tp[:], ALU.mult, ALU.subtract)
+
+        tw_turned = ps.tile([P, PACK, Q], F32, name="tw_turned", tag="score0")
+        for t in range(PACK):
+            nc.tensor.transpose(tw_turned[:, t, :], tw[:, t, :], ident[:])
+        gather_values(2)
+        gather_values(3)
+
+        early_codes = sb.tile([P, 3 * P], U32, name="early_codes", tag="slot4", align_bytes=64)
+        early_scales = sb.tile([P, 3 * P], U8, name="early_scales", align_bytes=64)
+        nc.vector.quantize_mx(
+            out=early_codes[:, : 2 * P].bitcast(FP8X4), scales=early_scales[:, : 2 * P],
+            in_=first_pair[:].rearrange("p c x -> p (c x)"),
+        )
+        w_grouped = sb.tile([P, Q, PACK], BF16, name="w_grouped", tag="slot5", align_bytes=64)
+        nc.vector.tensor_tensor(
+            w_grouped[:], tw_turned[:].rearrange("p t q -> p q t"),
+            slot_factor[:].unsqueeze(1).to_broadcast([P, Q, PACK]), ALU.mult,
+        )
+        nc.vector.quantize_mx(out=early_codes[:, 2 * P :].bitcast(FP8X4), scales=early_scales[:, 2 * P :], in_=v_grouped[2])
+        w_codes = sb.tile([P, Q], U32, name="w_codes", align_bytes=64)
+        w_scales = sb.tile([P, Q], U8, name="w_scales", align_bytes=64)
+        nc.vector.quantize_mx(out=w_codes[:].bitcast(FP8X4), scales=w_scales[:], in_=w_grouped[:].rearrange("p q t -> p (q t)"))
+        late_codes = sb.tile([P, P], U32, name="late_codes", tag="slot5", align_bytes=64)
+        late_scales = sb.tile([P, P], U8, name="late_scales", align_bytes=64)
+        nc.vector.quantize_mx(out=late_codes[:].bitcast(FP8X4), scales=late_scales[:], in_=v_grouped[3])
+
+        def multiply(result, codes, scales):
+            nc.tensor.matmul_mx(
+                out=result, lhsT=w_codes[:].bitcast(FP8X4), lhsT_scale=w_scales[:],
+                rhs=codes.bitcast(FP8X4), rhs_scale=scales, start=True, stop=True,
+            )
+
+        early = ps.tile([P, 3 * P], F32, name="early", tag="score1")
+        for cols in (slice(0, 2 * P), slice(2 * P, 3 * P)):
+            multiply(early[:, cols], early_codes[:, cols], early_scales[:, cols])
+        early_sb = sb.tile([P, 3 * P], F32, name="early_sb")
+        nc.scalar.copy(early_sb[:], early[:])
+        nc.sync.dma_start(out[:, : 3 * P], early_sb[:])
+
+        late = ps.tile([P, P], F32, name="late", tag="score2")
+        multiply(late[:], late_codes[:], late_scales[:])
+        late_sb = sb.tile([P, P], F32, name="late_sb")
+        nc.vector.tensor_copy(late_sb[:], late[:])
+        nc.sync.dma_start(out[:, 3 * P :], late_sb[:])

@@ -27,25 +27,28 @@ def tile_attend_ttgatedexp_kernel(tc, query, query2, dquery2, keys_words, keys_s
         sb = ctx.enter_context(tc.tile_pool(name="sb", bufs=1))
         ps = ctx.enter_context(tc.psum_pool(name="ps", bufs=1))
 
+        def reused(shape, dtype, name, slot):
+            return sb.tile(shape, dtype, name=name, tag=slot, align_bytes=64)
+
         offsets = sb.tile([P, I // 16], U16, name="offsets")
-        key_words = sb.tile([P, T], I32, name="key_words", tag="slot0", align_bytes=64)
+        key_words = reused([P, T], I32, "key_words", "after_keys")
         key_scales = sb.tile([P, T], U8, name="key_scales")
         warm_out = sb.tile([P, 1], F32, name="warm_out")
 
+        def load_queries(pool, n, rows):
+            raw = pool.tile([P, PACK, Q], F32, name=f"q_raw{n}", tag=f"after_cast{n}")
+            nc.sync.dma_start(raw[:], rows.rearrange("(p j) q -> p j q", j=PACK))
+            return raw
+
         nc.gpsimd.memset(key_scales[:].bitcast(I32), 0)
         nc.sync.dma_start(offsets[:], offs)
+        nc.sync.dma_start(key_words[:], keys_words[0].rearrange("p n t -> p (n t)").bitcast(I32))
+        q_raw = [load_queries(sb, 0, query2)]
         for quad in range(4):
             nc.scalar.dma_start(
                 key_scales[32 * quad : 32 * quad + 4, :].bitcast(I32),
                 keys_scales[0, 4 * quad : 4 * quad + 4, :].bitcast(I32),
             )
-        def load_queries(pool, n, rows):
-            raw = pool.tile([P, PACK, Q], F32, name=f"q_raw{n}")
-            nc.sync.dma_start(raw[:], rows.rearrange("(p j) q -> p j q", j=PACK))
-            return raw
-
-        nc.sync.dma_start(key_words[:], keys_words[0].rearrange("p n t -> p (n t)").bitcast(I32))
-        q_raw = [load_queries(sb, 0, query2)]
         with tc.tile_pool(name="head", bufs=1) as head:
             warm = head.tile([P, 1], F32, name="warm")
             nc.gpsimd.memset(warm[:], 0.0)
@@ -53,11 +56,11 @@ def tile_attend_ttgatedexp_kernel(tc, query, query2, dquery2, keys_words, keys_s
         later = ctx.enter_context(tc.tile_pool(name="later", bufs=1))
         q_raw.append(load_queries(later, 1, query))
         q_raw.append(load_queries(later, 2, dquery2))
-        slot_factor = later.tile([P, PACK], F32, name="slot_factor")
-        nc.sync.dma_start(slot_factor[:], slot_os[0].rearrange("(p t) -> p t", t=PACK))
+        os_rows = later.tile([P, PACK], F32, name="os_rows")
+        nc.sync.dma_start(os_rows[:], slot_os[0].rearrange("(p t) -> p t", t=PACK))
         v_raw = []
         for c in range(CHUNKS):
-            raw = later.tile([P, T], F32, name=f"v_raw{c}")
+            raw = later.tile([P, T], F32, name=f"v_raw{c}", tag=f"after_gather{c}", align_bytes=64)
             nc.sync.dma_start(raw[:], vals[P * c : P * (c + 1), :])
             v_raw.append(raw)
 
@@ -69,24 +72,34 @@ def tile_attend_ttgatedexp_kernel(tc, query, query2, dquery2, keys_words, keys_s
         k_codes = sb.tile([P, I], U32, name="k_codes", align_bytes=64)
         nc.vector.tensor_copy(k_codes[:], key_words[:].bitcast(U32).indirect(offsets[:]))
 
-        q_codes = sb.tile([P, 3, Q], U32, name="q_codes", tag="slot0", align_bytes=64)
+        q_codes = reused([P, 3, Q], U32, "q_codes", "after_keys")
         scores = []
         for n in range(3):
             grouped = sb.tile([P, Q, PACK], BF16, name=f"q_grouped{n}", align_bytes=64)
             nc.scalar.copy(grouped[:], q_raw[n][:].rearrange("p j q -> p q j"))
-            codes = q_codes[:, n, :]
-            scales = sb.tile([P, Q], U8, name=f"q_scales{n}", align_bytes=64)
-            nc.vector.quantize_mx(out=codes.bitcast(FP8X4), scales=scales[:], in_=grouped[:].rearrange("p q j -> p (q j)"))
+            codes = q_codes[:, n, :].bitcast(FP8X4)
+            scales = reused([P, Q], U8, f"q_scales{n}", f"after_score{n}")
+            nc.vector.quantize_mx(out=codes, scales=scales[:], in_=grouped[:].rearrange("p q j -> p (q j)"))
             bank = ps.tile([P, I], F32, name=f"score{n}", tag=f"score{n}")
             nc.tensor.matmul_mx(
-                out=bank[:], lhsT=codes.bitcast(FP8X4), lhsT_scale=scales[:],
+                out=bank[:], lhsT=codes, lhsT_scale=scales[:],
                 rhs=k_codes[:].bitcast(FP8X4), rhs_scale=k_scales[:], start=True, stop=True,
             )
             scores.append(bank)
         b_ps, a_ps, tb_ps = scores
 
-        def dealt(bank):
-            return bank[:].rearrange("q (s t) -> q t s", t=PACK)
+        def halves(rows):
+            return rows[:].rearrange("p (u g m) -> p g u m", u=2, m=16)
+
+        def in_order(rows):
+            return rows[:].rearrange("p (g u m) -> p g u m", u=2, m=16)
+
+        def turn(rows, grouped, name, bank):
+            pairs = rows[:].bitcast(F32)
+            turned = ps.tile([P, 2, P], F32, name=name, tag=bank)
+            for u in range(2):
+                nc.tensor.transpose(turned[:, u, :], pairs[:, P * u : P * (u + 1)], ident[:])
+            nc.scalar.copy(grouped.bitcast(F32).rearrange("p (x u) -> p x u", u=2), turned[:].rearrange("p u x -> p x u"))
 
         first_pair = sb.tile([P, 2, P * PACK], BF16, name="first_pair", align_bytes=64)
         v_grouped = [first_pair[:, 0, :], first_pair[:, 1, :]]
@@ -94,81 +107,74 @@ def tile_attend_ttgatedexp_kernel(tc, query, query2, dquery2, keys_words, keys_s
             single = sb.tile([P, P * PACK], BF16, name=f"v_grouped{c}", align_bytes=64)
             v_grouped.append(single[:])
 
-        def gather_values(c):
-            picked = sb.tile([P, I], BF16, name=f"v_picked{c}", tag=f"slot{c}", align_bytes=64)
-            nc.vector.tensor_copy(picked[:], v_raw[c][:].indirect(offsets[:]))
-            pairs = picked[:].bitcast(F32)
-            turned = ps.tile([P, 2, P], F32, name=f"v_turned{c}", tag=f"v_turned{c % 2}")
-            for u in range(2):
-                nc.tensor.transpose(turned[:, u, :], pairs[:, u : I // 2 : 2], ident[:])
-            nc.scalar.copy(
-                v_grouped[c].bitcast(F32).rearrange("p (e u) -> p e u", u=2),
-                turned[:].rearrange("p u e -> p e u"),
-            )
+        def gather_values(c, slot):
+            picked = reused([P, I], BF16, f"v_picked{c}", slot)
+            nc.vector.tensor_copy(halves(picked), v_raw[c][:].indirect(offsets[:]))
+            turn(picked, v_grouped[c], f"v_turned{c}", f"turned{c % 2}")
 
-        gt = sb.tile([P, PACK, P], F32, name="gt")
-        nc.scalar.activation(gt[:], dealt(b_ps), ACT.Sigmoid)
+        gt = later.tile([P, I], F32, name="gt", tag="after_cast2")
+        nc.scalar.activation(gt[:], b_ps[:], ACT.Sigmoid)
         neg_max = sb.tile([P, 1], F32, name="neg_max")
         nc.vector.tensor_reduce(neg_max[:], a_ps[:], mybir.AxisListType.X, ALU.max, negate=True)
-        neg_u = sb.tile([P, PACK, P], F32, name="neg_u", tag="slot1", align_bytes=64)
-        nc.vector.scalar_tensor_tensor(neg_u[:], gt[:], 1.0, dealt(tb_ps), ALU.subtract, ALU.mult)
-        r = sb.tile([P, PACK, P], F32, name="r")
-        nc.scalar.activation(r[:], dealt(a_ps), ACT.Exp, bias=neg_max[:])
-        gather_values(0)
-        p = sb.tile([P, PACK, P], F32, name="p")
+        r = reused([P, I], F32, "r", "after_p")
+        nc.scalar.activation(r[:], a_ps[:], ACT.Exp, bias=neg_max[:])
+        neg_u = sb.tile([P, I], F32, name="neg_u")
+        nc.vector.scalar_tensor_tensor(neg_u[:], gt[:], 1.0, tb_ps[:], ALU.subtract, ALU.mult)
+        gather_values(0, "after_score2")
+        os_spread = ps.tile([P, PACK, P], F32, name="os_spread", tag="score0")
+        for t in range(PACK):
+            nc.tensor.transpose(os_spread[:, t, :], os_rows[:, t : t + 1].to_broadcast([P, P]), ident[:])
+
+        p = sb.tile([P, I], F32, name="p")
         p_sum = sb.tile([P, 1], F32, name="p_sum")
         nc.vector.scalar_tensor_tensor(p[:], r[:], 1.0, gt[:], ALU.mult, ALU.mult, accum_out=p_sum[:])
+        neg_pos = reused([P, P, PACK], F32, "neg_pos", "after_w")
+        nc.vector.scalar_tensor_tensor(
+            neg_pos[:], p[:].rearrange("q (s t) -> q s t", t=PACK), -1.0, os_spread[:].rearrange("q t s -> q s t"), ALU.mult, ALU.mult,
+        )
         inv_sum = sb.tile([P, 1], F32, name="inv_sum")
         nc.vector.reciprocal(inv_sum[:], p_sum[:])
-        p_norm = sb.tile([P, PACK, P], F32, name="p_norm", tag="slot3", align_bytes=64)
-        nc.scalar.activation(p_norm[:], p[:], ACT.Copy, scale=inv_sum[:])
-        neg_tp = sb.tile([P, PACK, P], F32, name="neg_tp", tag="slot2", align_bytes=64)
-        neg_c = sb.tile([P, 1], F32, name="neg_c", tag="slot4", align_bytes=64)
-        nc.vector.scalar_tensor_tensor(neg_tp[:], p[:], inv_sum[:], neg_u[:], ALU.mult, ALU.mult, accum_out=neg_c[:])
-        gather_values(1)
-        tw = sb.tile([P, PACK, P], F32, name="tw")
-        nc.vector.scalar_tensor_tensor(tw[:], p_norm[:], neg_c[:], neg_tp[:], ALU.mult, ALU.subtract)
+        tp = reused([P, I], F32, "tp", "after_p")
+        tp_sum = reused([P, 1], F32, "tp_sum", "after_shift")
+        nc.vector.scalar_tensor_tensor(tp[:], p[:], -1.0, neg_u[:], ALU.mult, ALU.mult, accum_out=tp_sum[:])
+        shift = sb.tile([P, 1], F32, name="shift")
+        nc.vector.tensor_scalar(shift[:], tp_sum[:], inv_sum[:], inv_sum[:], ALU.mult, ALU.mult)
+        neg_v = reused([P, I], F32, "neg_v", "after_w2")
+        nc.scalar.activation(neg_v[:], neg_u[:], ACT.Identity, bias=shift[:], scale=inv_sum[:])
+        gather_values(1, "after_shift")
+        w_rows = sb.tile([P, I], BF16, name="w_rows")
+        nc.vector.tensor_tensor(halves(w_rows), in_order(neg_v), neg_pos[:].rearrange("q (g u a) t -> q g u (a t)", u=2, a=4), ALU.mult)
+        w_grouped = sb.tile([P, Q * PACK], BF16, name="w_grouped", align_bytes=64)
+        turn(w_rows, w_grouped[:], "w_turned", "score1")
+        gather_values(2, "after_w")
+        gather_values(3, "after_w2")
 
-        tw_turned = ps.tile([P, PACK, Q], F32, name="tw_turned", tag="score0")
-        for t in range(PACK):
-            nc.tensor.transpose(tw_turned[:, t, :], tw[:, t, :], ident[:])
-        gather_values(2)
-        gather_values(3)
+        out_codes = later.tile([P, E + Q], U32, name="out_codes", tag=f"after_gather{CHUNKS - 1}", align_bytes=64)
+        out_scales = sb.tile([P, E + Q], U8, name="out_scales", align_bytes=64)
+        first_cols, third_cols, last_cols, w_cols = slice(0, 2 * P), slice(2 * P, 3 * P), slice(3 * P, E), slice(E, E + Q)
 
-        early_codes = sb.tile([P, 3 * P], U32, name="early_codes", tag="slot4", align_bytes=64)
-        early_scales = sb.tile([P, 3 * P], U8, name="early_scales", align_bytes=64)
-        nc.vector.quantize_mx(
-            out=early_codes[:, : 2 * P].bitcast(FP8X4), scales=early_scales[:, : 2 * P],
-            in_=first_pair[:].rearrange("p c x -> p (c x)"),
-        )
-        w_grouped = sb.tile([P, Q, PACK], BF16, name="w_grouped", tag="slot5", align_bytes=64)
-        nc.vector.tensor_tensor(
-            w_grouped[:], tw_turned[:].rearrange("p t q -> p q t"),
-            slot_factor[:].unsqueeze(1).to_broadcast([P, Q, PACK]), ALU.mult,
-        )
-        nc.vector.quantize_mx(out=early_codes[:, 2 * P :].bitcast(FP8X4), scales=early_scales[:, 2 * P :], in_=v_grouped[2])
-        w_codes = sb.tile([P, Q], U32, name="w_codes", align_bytes=64)
-        w_scales = sb.tile([P, Q], U8, name="w_scales", align_bytes=64)
-        nc.vector.quantize_mx(out=w_codes[:].bitcast(FP8X4), scales=w_scales[:], in_=w_grouped[:].rearrange("p q t -> p (q t)"))
-        late_codes = sb.tile([P, P], U32, name="late_codes", tag="slot5", align_bytes=64)
-        late_scales = sb.tile([P, P], U8, name="late_scales", align_bytes=64)
-        nc.vector.quantize_mx(out=late_codes[:].bitcast(FP8X4), scales=late_scales[:], in_=v_grouped[3])
+        def quantize(cols, grouped):
+            nc.vector.quantize_mx(out=out_codes[:, cols].bitcast(FP8X4), scales=out_scales[:, cols], in_=grouped)
 
-        def multiply(result, codes, scales):
+        def multiply(result, cols):
             nc.tensor.matmul_mx(
-                out=result, lhsT=w_codes[:].bitcast(FP8X4), lhsT_scale=w_scales[:],
-                rhs=codes.bitcast(FP8X4), rhs_scale=scales, start=True, stop=True,
+                out=result, lhsT=out_codes[:, w_cols].bitcast(FP8X4), lhsT_scale=out_scales[:, w_cols],
+                rhs=out_codes[:, cols].bitcast(FP8X4), rhs_scale=out_scales[:, cols], start=True, stop=True,
             )
 
-        early = ps.tile([P, 3 * P], F32, name="early", tag="score1")
-        for cols in (slice(0, 2 * P), slice(2 * P, 3 * P)):
-            multiply(early[:, cols], early_codes[:, cols], early_scales[:, cols])
+        quantize(w_cols, w_grouped[:])
+        quantize(first_cols, first_pair[:].rearrange("p c x -> p (c x)"))
+        quantize(third_cols, v_grouped[2])
+        early = ps.tile([P, 3 * P], F32, name="early", tag="score0")
+        for cols in (first_cols, third_cols):
+            multiply(early[:, cols], cols)
+        quantize(last_cols, v_grouped[3])
+        late = ps.tile([P, P], F32, name="late", tag="score2")
+        multiply(late[:], last_cols)
+
         early_sb = sb.tile([P, 3 * P], F32, name="early_sb")
         nc.scalar.copy(early_sb[:], early[:])
         nc.sync.dma_start(out[:, : 3 * P], early_sb[:])
-
-        late = ps.tile([P, P], F32, name="late", tag="score2")
-        multiply(late[:], late_codes[:], late_scales[:])
         late_sb = sb.tile([P, P], F32, name="late_sb")
         nc.vector.tensor_copy(late_sb[:], late[:])
         nc.sync.dma_start(out[:, 3 * P :], late_sb[:])

@@ -1,7 +1,6 @@
 from contextlib import ExitStack
 
 import concourse.mybir as mybir
-from concourse.masks import make_identity
 
 D, E, T, I, Q = 512, 512, 2048, 512, 128
 FLOPS = 2 * Q * I * D * 3 + 2 * Q * I * E
@@ -33,7 +32,9 @@ def tile_attend_ttgatedexp_kernel(tc, query, query2, dquery2, keys_words, keys_s
         offsets = sb.tile([P, I // 16], U16, name="offsets")
         key_words = reused([P, T], I32, "key_words", "after_keys")
         key_scales = sb.tile([P, T], U8, name="key_scales")
+        warm = sb.tile([P, 1], F32, name="warm")
         warm_out = sb.tile([P, 1], F32, name="warm_out")
+        ident = sb.tile([P, P], F32, name="ident")
 
         def load_queries(pool, n, rows):
             raw = pool.tile([P, PACK, Q], F32, name=f"q_raw{n}", tag=f"after_cast{n}")
@@ -49,23 +50,24 @@ def tile_attend_ttgatedexp_kernel(tc, query, query2, dquery2, keys_words, keys_s
                 key_scales[32 * quad : 32 * quad + 4, :].bitcast(I32),
                 keys_scales[0, 4 * quad : 4 * quad + 4, :].bitcast(I32),
             )
+        nc.gpsimd.memset(warm[:], 0.0)
+        nc.scalar.activation(warm_out[:], warm[:], ACT.Sigmoid)
         with tc.tile_pool(name="head", bufs=1) as head:
-            warm = head.tile([P, 1], F32, name="warm")
-            nc.gpsimd.memset(warm[:], 0.0)
-            nc.scalar.activation(warm_out[:], warm[:], ACT.Sigmoid)
+            zeros = head.tile([P, P], F32, name="zeros")
+            nc.gpsimd.memset(zeros[:], 0.0)
+            nc.gpsimd.affine_select(
+                out=ident[:], in_=zeros[:], compare_op=ALU.not_equal, fill=1.0, base=0, pattern=[[-1, P]], channel_multiplier=1,
+            )
+        os_rows = sb.tile([P, PACK], F32, name="os_rows")
+        nc.gpsimd.dma_start(os_rows[:], slot_os[0].rearrange("(p t) -> p t", t=PACK))
         later = ctx.enter_context(tc.tile_pool(name="later", bufs=1))
         q_raw.append(load_queries(later, 1, query))
         q_raw.append(load_queries(later, 2, dquery2))
-        os_rows = later.tile([P, PACK], F32, name="os_rows")
-        nc.sync.dma_start(os_rows[:], slot_os[0].rearrange("(p t) -> p t", t=PACK))
         v_raw = []
         for c in range(CHUNKS):
             raw = later.tile([P, T], F32, name=f"v_raw{c}", tag=f"after_gather{c}", align_bytes=64)
             nc.sync.dma_start(raw[:], vals[P * c : P * (c + 1), :])
             v_raw.append(raw)
-
-        ident = sb.tile([P, P], F32, name="ident")
-        make_identity(nc, ident[:])
 
         k_scales = sb.tile([P, I], U8, name="k_scales", align_bytes=64)
         nc.vector.tensor_copy(k_scales[:], key_scales[:].indirect(offsets[:]))
@@ -114,38 +116,43 @@ def tile_attend_ttgatedexp_kernel(tc, query, query2, dquery2, keys_words, keys_s
 
         gt = later.tile([P, I], F32, name="gt", tag="after_cast2")
         nc.scalar.activation(gt[:], b_ps[:], ACT.Sigmoid)
-        neg_max = sb.tile([P, 1], F32, name="neg_max")
+        neg_max = reused([P, 1], F32, "neg_max", "after_exp")
         nc.vector.tensor_reduce(neg_max[:], a_ps[:], mybir.AxisListType.X, ALU.max, negate=True)
         r = reused([P, I], F32, "r", "after_p")
         nc.scalar.activation(r[:], a_ps[:], ACT.Exp, bias=neg_max[:])
-        neg_u = sb.tile([P, I], F32, name="neg_u")
+        neg_u = reused([P, I], F32, "neg_u", "after_w2")
         nc.vector.scalar_tensor_tensor(neg_u[:], gt[:], 1.0, tb_ps[:], ALU.subtract, ALU.mult)
         gather_values(0, "after_score2")
         os_spread = ps.tile([P, PACK, P], F32, name="os_spread", tag="score0")
         for t in range(PACK):
             nc.tensor.transpose(os_spread[:, t, :], os_rows[:, t : t + 1].to_broadcast([P, P]), ident[:])
 
+        rounded = reused([P, T], BF16, "v_rounded", "after_exp")
+        nc.scalar.activation(rounded[:], v_raw[1][:], ACT.Copy)
+        scalar_picked = sb.tile([P, I], BF16, name="v_picked1")
+        nc.scalar.activation(halves(scalar_picked), rounded[:].indirect(offsets[:]), ACT.Copy)
+
         p = sb.tile([P, I], F32, name="p")
         p_sum = sb.tile([P, 1], F32, name="p_sum")
         nc.vector.scalar_tensor_tensor(p[:], r[:], 1.0, gt[:], ALU.mult, ALU.mult, accum_out=p_sum[:])
-        neg_pos = reused([P, P, PACK], F32, "neg_pos", "after_w")
-        nc.vector.scalar_tensor_tensor(
-            neg_pos[:], p[:].rearrange("q (s t) -> q s t", t=PACK), -1.0, os_spread[:].rearrange("q t s -> q s t"), ALU.mult, ALU.mult,
-        )
         inv_sum = sb.tile([P, 1], F32, name="inv_sum")
         nc.vector.reciprocal(inv_sum[:], p_sum[:])
-        tp = reused([P, I], F32, "tp", "after_p")
-        tp_sum = reused([P, 1], F32, "tp_sum", "after_shift")
-        nc.vector.scalar_tensor_tensor(tp[:], p[:], -1.0, neg_u[:], ALU.mult, ALU.mult, accum_out=tp_sum[:])
-        shift = sb.tile([P, 1], F32, name="shift")
-        nc.vector.tensor_scalar(shift[:], tp_sum[:], inv_sum[:], inv_sum[:], ALU.mult, ALU.mult)
-        neg_v = reused([P, I], F32, "neg_v", "after_w2")
-        nc.scalar.activation(neg_v[:], neg_u[:], ACT.Identity, bias=shift[:], scale=inv_sum[:])
-        gather_values(1, "after_shift")
+        neg_tp = reused([P, I], F32, "neg_tp", "after_p")
+        neg_c = sb.tile([P, 1], F32, name="neg_c")
+        nc.vector.scalar_tensor_tensor(neg_tp[:], p[:], inv_sum[:], neg_u[:], ALU.mult, ALU.mult, accum_out=neg_c[:])
+        p_os = reused([P, I], F32, "p_os", "after_w")
+        nc.vector.scalar_tensor_tensor(
+            p_os[:].rearrange("q (s t) -> q s t", t=PACK), p[:].rearrange("q (s t) -> q s t", t=PACK), inv_sum[:],
+            os_spread[:].rearrange("q t s -> q s t"), ALU.mult, ALU.mult,
+        )
         w_rows = sb.tile([P, I], BF16, name="w_rows")
-        nc.vector.tensor_tensor(halves(w_rows), in_order(neg_v), neg_pos[:].rearrange("q (g u a) t -> q g u (a t)", u=2, a=4), ALU.mult)
+        for u in range(2):
+            nc.vector.scalar_tensor_tensor(
+                halves(w_rows)[:, :, u, :], in_order(neg_u)[:, :, u, :], neg_c[:], in_order(p_os)[:, :, u, :], ALU.subtract, ALU.mult,
+            )
         w_grouped = sb.tile([P, Q * PACK], BF16, name="w_grouped", align_bytes=64)
         turn(w_rows, w_grouped[:], "w_turned", "score1")
+        turn(scalar_picked, v_grouped[1], "v_turned1", "turned1")
         gather_values(2, "after_w")
         gather_values(3, "after_w2")
 
@@ -173,8 +180,8 @@ def tile_attend_ttgatedexp_kernel(tc, query, query2, dquery2, keys_words, keys_s
         multiply(late[:], last_cols)
 
         early_sb = sb.tile([P, 3 * P], F32, name="early_sb")
-        nc.scalar.copy(early_sb[:], early[:])
-        nc.sync.dma_start(out[:, : 3 * P], early_sb[:])
+        nc.scalar.activation(early_sb[:], early[:], ACT.Copy, scale=-1.0)
+        nc.scalar.dma_start(out[:, : 3 * P], early_sb[:])
         late_sb = sb.tile([P, P], F32, name="late_sb")
-        nc.vector.tensor_copy(late_sb[:], late[:])
+        nc.vector.tensor_scalar_mul(late_sb[:], late[:], -1.0)
         nc.sync.dma_start(out[:, 3 * P :], late_sb[:])

from contextlib import ExitStack

import concourse.mybir as mybir

D, E, T, I, Q = 512, 512, 2048, 512, 128
FLOPS = 2 * Q * I * D * 3 + 2 * Q * I * E

F32 = mybir.dt.float32
BF16 = mybir.dt.bfloat16
I32 = mybir.dt.int32
U32 = mybir.dt.uint32
U16 = mybir.dt.uint16
U8 = mybir.dt.uint8
FP8X4 = mybir.dt.float8_e4m3fn_x4
ALU = mybir.AluOpType
ACT = mybir.ActivationFunctionType

P = 128
PACK = 4
CHUNKS = E // P


def tile_attend_ttgatedexp_kernel(tc, query, query2, dquery2, keys_words, keys_scales, slot_os, vals, offs, out):
    nc = tc.nc
    with ExitStack() as ctx:
        sb = ctx.enter_context(tc.tile_pool(name="sb", bufs=1))
        ps = ctx.enter_context(tc.psum_pool(name="ps", bufs=1))

        def reused(shape, dtype, name, slot):
            return sb.tile(shape, dtype, name=name, tag=slot, align_bytes=64)

        offsets = sb.tile([P, I // 16], U16, name="offsets")
        key_words = reused([P, T], I32, "key_words", "after_keys")
        key_scales = sb.tile([P, T], U8, name="key_scales")
        warm = sb.tile([P, 1], F32, name="warm")
        warm_out = sb.tile([P, 1], F32, name="warm_out")
        ident = sb.tile([P, P], F32, name="ident")

        def load_queries(pool, n, rows):
            raw = pool.tile([P, PACK, Q], F32, name=f"q_raw{n}", tag=f"after_cast{n}")
            nc.sync.dma_start(raw[:], rows.rearrange("(p j) q -> p j q", j=PACK))
            return raw

        nc.gpsimd.memset(key_scales[:].bitcast(I32), 0)
        nc.sync.dma_start(offsets[:], offs)
        nc.sync.dma_start(key_words[:], keys_words[0].rearrange("p n t -> p (n t)").bitcast(I32))
        q_raw = [load_queries(sb, 0, query2)]
        for quad in range(4):
            nc.scalar.dma_start(
                key_scales[32 * quad : 32 * quad + 4, :].bitcast(I32),
                keys_scales[0, 4 * quad : 4 * quad + 4, :].bitcast(I32),
            )
        nc.gpsimd.memset(warm[:], 0.0)
        nc.scalar.activation(warm_out[:], warm[:], ACT.Sigmoid)
        with tc.tile_pool(name="head", bufs=1) as head:
            zeros = head.tile([P, P], F32, name="zeros")
            nc.gpsimd.memset(zeros[:], 0.0)
            nc.gpsimd.affine_select(
                out=ident[:], in_=zeros[:], compare_op=ALU.not_equal, fill=1.0, base=0, pattern=[[-1, P]], channel_multiplier=1,
            )
        os_rows = sb.tile([P, PACK], F32, name="os_rows")
        nc.gpsimd.dma_start(os_rows[:], slot_os[0].rearrange("(p t) -> p t", t=PACK))
        later = ctx.enter_context(tc.tile_pool(name="later", bufs=1))
        q_raw.append(load_queries(later, 1, query))
        q_raw.append(load_queries(later, 2, dquery2))
        v_raw = []
        for c in range(CHUNKS):
            raw = later.tile([P, T], F32, name=f"v_raw{c}", tag=f"after_gather{c}", align_bytes=64)
            nc.sync.dma_start(raw[:], vals[P * c : P * (c + 1), :])
            v_raw.append(raw)

        k_scales = sb.tile([P, I], U8, name="k_scales", align_bytes=64)
        nc.vector.tensor_copy(k_scales[:], key_scales[:].indirect(offsets[:]))
        k_codes = sb.tile([P, I], U32, name="k_codes", align_bytes=64)
        nc.vector.tensor_copy(k_codes[:], key_words[:].bitcast(U32).indirect(offsets[:]))

        q_codes = reused([P, 3, Q], U32, "q_codes", "after_keys")
        scores = []
        for n in range(3):
            grouped = sb.tile([P, Q, PACK], BF16, name=f"q_grouped{n}", align_bytes=64)
            nc.scalar.copy(grouped[:], q_raw[n][:].rearrange("p j q -> p q j"))
            codes = q_codes[:, n, :].bitcast(FP8X4)
            scales = reused([P, Q], U8, f"q_scales{n}", f"after_score{n}")
            nc.vector.quantize_mx(out=codes, scales=scales[:], in_=grouped[:].rearrange("p q j -> p (q j)"))
            bank = ps.tile([P, I], F32, name=f"score{n}", tag=f"score{n}")
            nc.tensor.matmul_mx(
                out=bank[:], lhsT=codes, lhsT_scale=scales[:],
                rhs=k_codes[:].bitcast(FP8X4), rhs_scale=k_scales[:], start=True, stop=True,
            )
            scores.append(bank)
        b_ps, a_ps, tb_ps = scores

        def halves(rows):
            return rows[:].rearrange("p (u g m) -> p g u m", u=2, m=16)

        def in_order(rows):
            return rows[:].rearrange("p (g u m) -> p g u m", u=2, m=16)

        def turn(rows, grouped, name, bank):
            pairs = rows[:].bitcast(F32)
            turned = ps.tile([P, 2, P], F32, name=name, tag=bank)
            for u in range(2):
                nc.tensor.transpose(turned[:, u, :], pairs[:, P * u : P * (u + 1)], ident[:])
            nc.scalar.copy(grouped.bitcast(F32).rearrange("p (x u) -> p x u", u=2), turned[:].rearrange("p u x -> p x u"))

        first_pair = sb.tile([P, 2, P * PACK], BF16, name="first_pair", align_bytes=64)
        v_grouped = [first_pair[:, 0, :], first_pair[:, 1, :]]
        for c in range(2, CHUNKS):
            single = sb.tile([P, P * PACK], BF16, name=f"v_grouped{c}", align_bytes=64)
            v_grouped.append(single[:])

        def gather_values(c, slot):
            picked = reused([P, I], BF16, f"v_picked{c}", slot)
            nc.vector.tensor_copy(halves(picked), v_raw[c][:].indirect(offsets[:]))
            turn(picked, v_grouped[c], f"v_turned{c}", f"turned{c % 2}")

        gt = later.tile([P, I], F32, name="gt", tag="after_cast2")
        nc.scalar.activation(gt[:], b_ps[:], ACT.Sigmoid)
        neg_max = reused([P, 1], F32, "neg_max", "after_exp")
        nc.vector.tensor_reduce(neg_max[:], a_ps[:], mybir.AxisListType.X, ALU.max, negate=True)
        r = reused([P, I], F32, "r", "after_p")
        nc.scalar.activation(r[:], a_ps[:], ACT.Exp, bias=neg_max[:])
        neg_u = reused([P, I], F32, "neg_u", "after_w2")
        nc.vector.scalar_tensor_tensor(neg_u[:], gt[:], 1.0, tb_ps[:], ALU.subtract, ALU.mult)
        gather_values(0, "after_score2")
        os_spread = ps.tile([P, PACK, P], F32, name="os_spread", tag="score0")
        for t in range(PACK):
            nc.tensor.transpose(os_spread[:, t, :], os_rows[:, t : t + 1].to_broadcast([P, P]), ident[:])

        rounded = reused([P, T], BF16, "v_rounded", "after_exp")
        nc.scalar.activation(rounded[:], v_raw[1][:], ACT.Copy)
        scalar_picked = sb.tile([P, I], BF16, name="v_picked1")
        nc.scalar.activation(halves(scalar_picked), rounded[:].indirect(offsets[:]), ACT.Copy)

        p = sb.tile([P, I], F32, name="p")
        p_sum = sb.tile([P, 1], F32, name="p_sum")
        nc.vector.scalar_tensor_tensor(p[:], r[:], 1.0, gt[:], ALU.mult, ALU.mult, accum_out=p_sum[:])
        inv_sum = sb.tile([P, 1], F32, name="inv_sum")
        nc.vector.reciprocal(inv_sum[:], p_sum[:])
        neg_tp = reused([P, I], F32, "neg_tp", "after_p")
        neg_c = sb.tile([P, 1], F32, name="neg_c")
        nc.vector.scalar_tensor_tensor(neg_tp[:], p[:], inv_sum[:], neg_u[:], ALU.mult, ALU.mult, accum_out=neg_c[:])
        p_os = reused([P, I], F32, "p_os", "after_w")
        nc.vector.scalar_tensor_tensor(
            p_os[:].rearrange("q (s t) -> q s t", t=PACK), p[:].rearrange("q (s t) -> q s t", t=PACK), inv_sum[:],
            os_spread[:].rearrange("q t s -> q s t"), ALU.mult, ALU.mult,
        )
        w_rows = sb.tile([P, I], BF16, name="w_rows")
        for u in range(2):
            nc.vector.scalar_tensor_tensor(
                halves(w_rows)[:, :, u, :], in_order(neg_u)[:, :, u, :], neg_c[:], in_order(p_os)[:, :, u, :], ALU.subtract, ALU.mult,
            )
        w_grouped = sb.tile([P, Q * PACK], BF16, name="w_grouped", align_bytes=64)
        turn(w_rows, w_grouped[:], "w_turned", "score1")
        turn(scalar_picked, v_grouped[1], "v_turned1", "turned1")
        gather_values(2, "after_w")
        gather_values(3, "after_w2")

        out_codes = later.tile([P, E + Q], U32, name="out_codes", tag=f"after_gather{CHUNKS - 1}", align_bytes=64)
        out_scales = sb.tile([P, E + Q], U8, name="out_scales", align_bytes=64)
        first_cols, third_cols, last_cols, w_cols = slice(0, 2 * P), slice(2 * P, 3 * P), slice(3 * P, E), slice(E, E + Q)

        def quantize(cols, grouped):
            nc.vector.quantize_mx(out=out_codes[:, cols].bitcast(FP8X4), scales=out_scales[:, cols], in_=grouped)

        def multiply(result, cols):
            nc.tensor.matmul_mx(
                out=result, lhsT=out_codes[:, w_cols].bitcast(FP8X4), lhsT_scale=out_scales[:, w_cols],
                rhs=out_codes[:, cols].bitcast(FP8X4), rhs_scale=out_scales[:, cols], start=True, stop=True,
            )

        quantize(w_cols, w_grouped[:])
        quantize(first_cols, first_pair[:].rearrange("p c x -> p (c x)"))
        quantize(third_cols, v_grouped[2])
        early = ps.tile([P, 3 * P], F32, name="early", tag="score0")
        for cols in (first_cols, third_cols):
            multiply(early[:, cols], cols)
        quantize(last_cols, v_grouped[3])
        late = ps.tile([P, P], F32, name="late", tag="score2")
        multiply(late[:], last_cols)

        early_sb = sb.tile([P, 3 * P], F32, name="early_sb")
        nc.scalar.activation(early_sb[:], early[:], ACT.Copy, scale=-1.0)
        nc.scalar.dma_start(out[:, : 3 * P], early_sb[:])
        late_sb = sb.tile([P, P], F32, name="late_sb")
        nc.vector.tensor_scalar_mul(late_sb[:], late[:], -1.0)
        nc.sync.dma_start(out[:, 3 * P :], late_sb[:])
